import numpy as np
CORES = [3,11,19,27,35,43,51,59,67,75,83,91,99,107,115,123,131,139,147,155,163,171,179,187,195,203,211,219,227,235,243,251]
N = 32
def setup_inputs(rng):
    return {"x": rng.standard_normal((N, 128, 1024), dtype=np.float32)}
def reference(x):
    s = x.sum(axis=0, dtype=np.float64).astype(x.dtype)
    b = 1024 // N
    return {"y": np.stack([s[:, r * b:(r + 1) * b] for r in range(N)])}

@@ -1,0 +1,53 @@
+from concourse.bass import RemoteDMATransfer, DstId
+NR = 32
+BW = 32
+QW = 256
+COL = 1
+HELP = [7, 6, 2]
+SCRATCH = {'xs': ('sbuf', [128, NR * BW], 'float32'), 'rq': ('sbuf', [128, QW], 'float32'), 'land': ('dram', [NR, 128, BW], 'float32'), 'fin': ('dram', [128, BW], 'float32')}
+SEMAPHORES = ['ld0', 'ld1', 'ld2', 'ld3', 'st', 'sent', 'rl', 'arr', 'af']
+
+def quarter(c, l):
+    return c >> 3 ^ {3: 0, 2: 1, 7: 2, 6: 3}[l]
+
+def send(g, core, T, topo, src, base, q):
+    c = core // 8
+    trs = []
+    for i in range(8):
+        k = (i + c) % 8
+        rid, pid = topo.addr(8 * (8 * q + k) + COL, core)
+        trs.append(RemoteDMATransfer(dst_ids=[DstId(rid=rid, pnc=pid)], dma_engine_mask=1 << i, remote_sem=T.sem.arr, src=src[:, base + k * BW:base + (k + 1) * BW], dst=T.land[c]))
+    g.remote_dma_fused(trs, local_sem=T.sem.sent)
+    return 8
+
+def rank_program(g, core, T, topo):
+    c, l = (core // 8, core % 8)
+    if l == 3:
+        lds = [T.sem.ld0, T.sem.ld1, T.sem.ld2, T.sem.ld3]
+        who = HELP + [3]
+        for i, h in enumerate(who):
+            a = quarter(c, h) * QW
+            g.dma_start(T.xs[:, a:a + QW], T.x[:, a:a + QW]).then_inc(lds[i], 16)
+        sent = 0
+        for i, h in enumerate(who):
+            a = quarter(c, h) * QW
+            g.wait_ge(lds[i], 16)
+            if h != 3:
+                rid, pid = topo.addr(8 * c + h, core)
+                g.remote_dma(T.rq[:], T.xs[:, a:a + QW], T.sem.rl, T.sem.sent, pid, rid, 65535)
+                sent += 16
+            else:
+                sent += send(g, core, T, topo, T.xs, a, quarter(c, 3))
+        g.wait_ge(T.sem.af, 16)
+        g.dma_start(T.y[:], T.fin[:]).then_inc(T.sem.st, 16)
+        g.wait_ge(T.sem.st, 16)
+        g.wait_ge(T.sem.sent, sent)
+    elif l in HELP:
+        g.wait_ge(T.sem.rl, 16)
+        sent = send(g, core, T, topo, T.rq, 0, quarter(c, l))
+        g.wait_ge(T.sem.sent, sent)
+    elif l == COL:
+        g.wait_ge(T.sem.arr, NR)
+        rid, pid = topo.addr(8 * c + 3, core)
+        g.remote_dma_fused([RemoteDMATransfer(dst_ids=[DstId(rid=rid, pnc=pid)], dma_engine_mask=65535, remote_sem=T.sem.af, srcs=[T.land[s] for s in range(NR)], dsts=[T.fin[:]], alu_op=1)], local_sem=T.sem.sent)
+        g.wait_ge(T.sem.sent, 16)

@@ -27,7 +27,10 @@ def rank_program(g, core, T, topo):
         who = HELP + [3]
         for i, h in enumerate(who):
             a = quarter(c, h) * QW
-            g.dma_start(T.xs[:, a:a + QW], T.x[:, a:a + QW]).then_inc(lds[i], 16)
+            q = g.sync if i % 2 == 0 else g.scalar
+            q.dma_start(T.xs[:, a:a + QW], T.x[:, a:a + QW]).then_inc(lds[i], 16)
+        g.sync.wait_ge(T.sem.af, 16)
+        g.sync.dma_start(T.y[:], T.fin[:]).then_inc(T.sem.st, 16)
         sent = 0
         for i, h in enumerate(who):
             a = quarter(c, h) * QW
@@ -38,10 +41,8 @@ def rank_program(g, core, T, topo):
                 sent += 16
             else:
                 sent += send(g, core, T, topo, T.xs, a, quarter(c, 3))
-        g.wait_ge(T.sem.af, 16)
-        g.dma_start(T.y[:], T.fin[:]).then_inc(T.sem.st, 16)
-        g.wait_ge(T.sem.st, 16)
         g.wait_ge(T.sem.sent, sent)
+        g.wait_ge(T.sem.st, 16)
     elif l in HELP:
         g.wait_ge(T.sem.rl, 16)
         sent = send(g, core, T, topo, T.rq, 0, quarter(c, l))

@@ -2,23 +2,32 @@ from concourse.bass import RemoteDMATransfer, DstId
 NR = 32
 BW = 32
 QW = 256
-COL = 1
 HELP = [7, 6, 2]
-SCRATCH = {'xs': ('sbuf', [128, NR * BW], 'float32'), 'rq': ('sbuf', [128, QW], 'float32'), 'land': ('dram', [NR, 128, BW], 'float32'), 'fin': ('dram', [128, BW], 'float32')}
-SEMAPHORES = ['ld0', 'ld1', 'ld2', 'ld3', 'st', 'sent', 'rl', 'arr', 'af']
+IDX = {3: 0, 2: 1, 7: 2, 6: 3}
+COLL = {3: 1, 2: 0, 7: 4, 6: 5}
+FIN = 2
+SCRATCH = {'xs': ('sbuf', [128, NR * BW], 'float32'), 'rq': ('sbuf', [128, QW], 'float32'),
+           'land': ('dram', [8, 128, BW], 'float32'), 'part': ('dram', [4, 128, BW], 'float32'),
+           'fin': ('dram', [128, BW], 'float32')}
+SEMAPHORES = ['ld0', 'ld1', 'ld2', 'ld3', 'st', 'sent', 'rl', 'arr', 'pf', 'af']
 
 def quarter(c, l):
-    return c >> 3 ^ {3: 0, 2: 1, 7: 2, 6: 3}[l]
+    return c >> 3 ^ IDX[l]
 
 def send(g, core, T, topo, src, base, q):
-    c = core // 8
+    c, l = core // 8, core % 8
     trs = []
     for i in range(8):
         k = (i + c) % 8
-        rid, pid = topo.addr(8 * (8 * q + k) + COL, core)
-        trs.append(RemoteDMATransfer(dst_ids=[DstId(rid=rid, pnc=pid)], dma_engine_mask=1 << i, remote_sem=T.sem.arr, src=src[:, base + k * BW:base + (k + 1) * BW], dst=T.land[c]))
+        rid, pid = topo.addr(8 * (8 * q + k) + COLL[l], core)
+        trs.append(RemoteDMATransfer(dst_ids=[DstId(rid=rid, pnc=pid)], dma_engine_mask=1 << i, remote_sem=T.sem.arr, src=src[:, base + k * BW:base + (k + 1) * BW], dst=T.land[c % 8]))
     g.remote_dma_fused(trs, local_sem=T.sem.sent)
     return 8
+
+def fold(g, core, T, topo, dst_core, srcs, dst, sem):
+    rid, pid = topo.addr(dst_core, core)
+    g.remote_dma_fused([RemoteDMATransfer(dst_ids=[DstId(rid=rid, pnc=pid)], dma_engine_mask=65535, remote_sem=sem, srcs=srcs, dsts=[dst], alu_op=1)], local_sem=T.sem.sent)
+    return 16
 
 def rank_program(g, core, T, topo):
     c, l = (core // 8, core % 8)
@@ -46,9 +55,12 @@ def rank_program(g, core, T, topo):
     elif l in HELP:
         g.wait_ge(T.sem.rl, 16)
         sent = send(g, core, T, topo, T.rq, 0, quarter(c, l))
+        if l == FIN:
+            g.wait_ge(T.sem.pf, 64)
+            sent += fold(g, core, T, topo, 8 * c + 3, [T.part[j] for j in range(4)], T.fin[:], T.sem.af)
         g.wait_ge(T.sem.sent, sent)
-    elif l == COL:
-        g.wait_ge(T.sem.arr, NR)
-        rid, pid = topo.addr(8 * c + 3, core)
-        g.remote_dma_fused([RemoteDMATransfer(dst_ids=[DstId(rid=rid, pnc=pid)], dma_engine_mask=65535, remote_sem=T.sem.af, srcs=[T.land[s] for s in range(NR)], dsts=[T.fin[:]], alu_op=1)], local_sem=T.sem.sent)
-        g.wait_ge(T.sem.sent, 16)
+    else:
+        j = [1, 0, 4, 5].index(l)
+        g.wait_ge(T.sem.arr, 8)
+        sent = fold(g, core, T, topo, 8 * c + FIN, [T.land[s] for s in range(8)], T.part[j], T.sem.pf)
+        g.wait_ge(T.sem.sent, sent)

@@ -1,66 +1,86 @@
 from concourse.bass import RemoteDMATransfer, DstId
-NR = 32
 BW = 32
+EW = 128
 QW = 256
-HELP = [7, 6, 2]
-IDX = {3: 0, 2: 1, 7: 2, 6: 3}
-COLL = {3: 1, 2: 0, 7: 4, 6: 5}
-FIN = 2
-SCRATCH = {'xs': ('sbuf', [128, NR * BW], 'float32'), 'rq': ('sbuf', [128, QW], 'float32'),
-           'land': ('dram', [8, 128, BW], 'float32'), 'part': ('dram', [4, 128, BW], 'float32'),
-           'fin': ('dram', [128, BW], 'float32')}
-SEMAPHORES = ['ld0', 'ld1', 'ld2', 'ld3', 'st', 'sent', 'rl', 'arr', 'pf', 'af']
+CORELIST = [3, 2, 1, 0, 7, 6, 5, 4]
+OWN = [0, 4]
+PROXY = [2, 3, 6, 7]
+FIN = 1
+SCRATCH = {'xs': ('sbuf', [128, 1024], 'float32'), 'rq': ('sbuf', [128, EW], 'float32'),
+           'land': ('dram', [8, 128, BW], 'float32'), 'pland': ('dram', [4, 128, BW], 'float32'),
+           'part': ('dram', [6, 128, BW], 'float32'), 'fin': ('dram', [128, BW], 'float32')}
+SEMAPHORES = ['ld0', 'ld1', 'ld2', 'ld3', 'st', 'sent', 'rl', 'arr', 'parr', 'pf', 'af']
 
-def quarter(c, l):
-    return c >> 3 ^ IDX[l]
 
-def send(g, core, T, topo, src, base, q):
+def did(topo, core, dst_core):
+    rid, pid = topo.addr(dst_core, core)
+    return DstId(rid=rid, pnc=pid)
+
+
+def send(g, core, T, topo, src, base):
     c, l = core // 8, core % 8
+    s = CORELIST.index(l)
+    e = s ^ (c >> 2)
     trs = []
-    for i in range(8):
-        k = (i + c) % 8
-        rid, pid = topo.addr(8 * (8 * q + k) + COLL[l], core)
-        trs.append(RemoteDMATransfer(dst_ids=[DstId(rid=rid, pnc=pid)], dma_engine_mask=1 << i, remote_sem=T.sem.arr, src=src[:, base + k * BW:base + (k + 1) * BW], dst=T.land[c % 8]))
+    for k in range(4):
+        d = 4 * e + k
+        sl = src[:, base + k * BW:base + (k + 1) * BW]
+        if not (d ^ c) & 1:
+            trs.append(RemoteDMATransfer(dst_ids=[did(topo, core, 8 * d + OWN[s >> 2])], dma_engine_mask=3 << (2 * k), remote_sem=T.sem.arr,
+                                         src=sl, dst=T.land[((c >> 2) & 3) * 2 + ((c >> 1) & 1)]))
+        else:
+            trs.append(RemoteDMATransfer(dst_ids=[did(topo, core, 8 * (d ^ 1) + PROXY[s >> 1])], dma_engine_mask=3 << (2 * k), remote_sem=T.sem.parr,
+                                         src=sl, dst=T.pland[(s & 1) * 2 + ((c >> 1) & 1)]))
     g.remote_dma_fused(trs, local_sem=T.sem.sent)
     return 8
 
-def fold(g, core, T, topo, dst_core, srcs, dst, sem):
-    rid, pid = topo.addr(dst_core, core)
-    g.remote_dma_fused([RemoteDMATransfer(dst_ids=[DstId(rid=rid, pnc=pid)], dma_engine_mask=65535, remote_sem=sem, srcs=srcs, dsts=[dst], alu_op=1)], local_sem=T.sem.sent)
-    return 16
+
+def fold(g, core, T, topo, dst_core, srcs, dst, sem, mask):
+    g.remote_dma_fused([RemoteDMATransfer(dst_ids=[did(topo, core, dst_core)], dma_engine_mask=mask, remote_sem=sem, srcs=srcs, dsts=[dst], alu_op=1)], local_sem=T.sem.sent)
+    return bin(mask).count('1')
+
 
 def rank_program(g, core, T, topo):
     c, l = (core // 8, core % 8)
+    s = CORELIST.index(l)
+    sent = 0
     if l == 3:
         lds = [T.sem.ld0, T.sem.ld1, T.sem.ld2, T.sem.ld3]
-        who = HELP + [3]
-        for i, h in enumerate(who):
-            a = quarter(c, h) * QW
-            q = g.sync if i % 2 == 0 else g.scalar
-            q.dma_start(T.xs[:, a:a + QW], T.x[:, a:a + QW]).then_inc(lds[i], 16)
+        order = [2, 1, 3, 0]
+        for n, i in enumerate(order):
+            a = ((c >> 3) ^ i) * QW
+            q = g.sync if n % 2 == 0 else g.scalar
+            q.dma_start(T.xs[:, a:a + QW], T.x[:, a:a + QW]).then_inc(lds[n], 16)
         g.sync.wait_ge(T.sem.af, 16)
         g.sync.dma_start(T.y[:], T.fin[:]).then_inc(T.sem.st, 16)
-        sent = 0
-        for i, h in enumerate(who):
-            a = quarter(c, h) * QW
-            g.wait_ge(lds[i], 16)
-            if h != 3:
-                rid, pid = topo.addr(8 * c + h, core)
-                g.remote_dma(T.rq[:], T.xs[:, a:a + QW], T.sem.rl, T.sem.sent, pid, rid, 65535)
+        for n, i in enumerate(order):
+            g.wait_ge(lds[n], 16)
+            if i:
+                trs = []
+                for b in range(2):
+                    a = ((2 * i + b) ^ (c >> 2)) * EW
+                    trs.append(RemoteDMATransfer(dst_ids=[did(topo, core, 8 * c + CORELIST[2 * i + b])], dma_engine_mask=255 << (8 * b),
+                                                 remote_sem=T.sem.rl, src=T.xs[:, a:a + EW], dst=T.rq[:]))
+                g.remote_dma_fused(trs, local_sem=T.sem.sent)
                 sent += 16
             else:
-                sent += send(g, core, T, topo, T.xs, a, quarter(c, 3))
-        g.wait_ge(T.sem.sent, sent)
-        g.wait_ge(T.sem.st, 16)
-    elif l in HELP:
-        g.wait_ge(T.sem.rl, 16)
-        sent = send(g, core, T, topo, T.rq, 0, quarter(c, l))
-        if l == FIN:
-            g.wait_ge(T.sem.pf, 64)
-            sent += fold(g, core, T, topo, 8 * c + 3, [T.part[j] for j in range(4)], T.fin[:], T.sem.af)
-        g.wait_ge(T.sem.sent, sent)
+                a = (1 ^ (c >> 2)) * EW
+                rid, pid = topo.addr(8 * c + CORELIST[1], core)
+                g.remote_dma(T.rq[:], T.xs[:, a:a + EW], T.sem.rl, T.sem.sent, pid, rid, 65535)
+                sent += 16
+                sent += send(g, core, T, topo, T.xs, (c >> 2) * EW)
     else:
-        j = [1, 0, 4, 5].index(l)
-        g.wait_ge(T.sem.arr, 8)
-        sent = fold(g, core, T, topo, 8 * c + FIN, [T.land[s] for s in range(8)], T.part[j], T.sem.pf)
-        g.wait_ge(T.sem.sent, sent)
+        g.wait_ge(T.sem.rl, 16 if s == 1 else 8)
+        sent += send(g, core, T, topo, T.rq, 0)
+    if l in OWN:
+        g.wait_ge(T.sem.arr, 16)
+        sent += fold(g, core, T, topo, 8 * c + FIN, [T.land[j] for j in range(8)], T.part[OWN.index(l)], T.sem.pf, 65535)
+    elif l in PROXY:
+        g.wait_ge(T.sem.parr, 8)
+        sent += fold(g, core, T, topo, 8 * (c ^ 1) + FIN, [T.pland[j] for j in range(4)], T.part[2 + PROXY.index(l)], T.sem.pf, 255)
+    elif l == FIN:
+        g.wait_ge(T.sem.pf, 64)
+        sent += fold(g, core, T, topo, 8 * c + 3, [T.part[j] for j in range(6)], T.fin[:], T.sem.af, 65535)
+    g.wait_ge(T.sem.sent, sent)
+    if l == 3:
+        g.wait_ge(T.sem.st, 16)

from concourse.bass import RemoteDMATransfer, DstId
BW = 32
EW = 128
QW = 256
CORELIST = [3, 2, 1, 0, 7, 6, 5, 4]
OWN = [0, 4]
PROXY = [2, 3, 6, 7]
FIN = 1
SCRATCH = {'xs': ('sbuf', [128, 1024], 'float32'), 'rq': ('sbuf', [128, EW], 'float32'),
           'land': ('dram', [8, 128, BW], 'float32'), 'pland': ('dram', [4, 128, BW], 'float32'),
           'part': ('dram', [6, 128, BW], 'float32'), 'fin': ('dram', [128, BW], 'float32')}
SEMAPHORES = ['ld0', 'ld1', 'ld2', 'ld3', 'st', 'sent', 'rl', 'arr', 'parr', 'pf', 'af']


def did(topo, core, dst_core):
    rid, pid = topo.addr(dst_core, core)
    return DstId(rid=rid, pnc=pid)


def send(g, core, T, topo, src, base):
    c, l = core // 8, core % 8
    s = CORELIST.index(l)
    e = s ^ (c >> 2)
    trs = []
    for k in range(4):
        d = 4 * e + k
        sl = src[:, base + k * BW:base + (k + 1) * BW]
        if not (d ^ c) & 1:
            trs.append(RemoteDMATransfer(dst_ids=[did(topo, core, 8 * d + OWN[s >> 2])], dma_engine_mask=3 << (2 * k), remote_sem=T.sem.arr,
                                         src=sl, dst=T.land[((c >> 2) & 3) * 2 + ((c >> 1) & 1)]))
        else:
            trs.append(RemoteDMATransfer(dst_ids=[did(topo, core, 8 * (d ^ 1) + PROXY[s >> 1])], dma_engine_mask=3 << (2 * k), remote_sem=T.sem.parr,
                                         src=sl, dst=T.pland[(s & 1) * 2 + ((c >> 1) & 1)]))
    g.remote_dma_fused(trs, local_sem=T.sem.sent)
    return 8


def fold(g, core, T, topo, dst_core, srcs, dst, sem, mask):
    g.remote_dma_fused([RemoteDMATransfer(dst_ids=[did(topo, core, dst_core)], dma_engine_mask=mask, remote_sem=sem, srcs=srcs, dsts=[dst], alu_op=1)], local_sem=T.sem.sent)
    return bin(mask).count('1')


def rank_program(g, core, T, topo):
    c, l = (core // 8, core % 8)
    s = CORELIST.index(l)
    sent = 0
    if l == 3:
        lds = [T.sem.ld0, T.sem.ld1, T.sem.ld2, T.sem.ld3]
        order = [2, 1, 3, 0]
        for n, i in enumerate(order):
            a = ((c >> 3) ^ i) * QW
            q = g.sync if n % 2 == 0 else g.scalar
            q.dma_start(T.xs[:, a:a + QW], T.x[:, a:a + QW]).then_inc(lds[n], 16)
        g.sync.wait_ge(T.sem.af, 16)
        g.sync.dma_start(T.y[:], T.fin[:]).then_inc(T.sem.st, 16)
        for n, i in enumerate(order):
            g.wait_ge(lds[n], 16)
            if i:
                trs = []
                for b in range(2):
                    a = ((2 * i + b) ^ (c >> 2)) * EW
                    trs.append(RemoteDMATransfer(dst_ids=[did(topo, core, 8 * c + CORELIST[2 * i + b])], dma_engine_mask=255 << (8 * b),
                                                 remote_sem=T.sem.rl, src=T.xs[:, a:a + EW], dst=T.rq[:]))
                g.remote_dma_fused(trs, local_sem=T.sem.sent)
                sent += 16
            else:
                a = (1 ^ (c >> 2)) * EW
                rid, pid = topo.addr(8 * c + CORELIST[1], core)
                g.remote_dma(T.rq[:], T.xs[:, a:a + EW], T.sem.rl, T.sem.sent, pid, rid, 65535)
                sent += 16
                sent += send(g, core, T, topo, T.xs, (c >> 2) * EW)
    else:
        g.wait_ge(T.sem.rl, 16 if s == 1 else 8)
        sent += send(g, core, T, topo, T.rq, 0)
    if l in OWN:
        g.wait_ge(T.sem.arr, 16)
        sent += fold(g, core, T, topo, 8 * c + FIN, [T.land[j] for j in range(8)], T.part[OWN.index(l)], T.sem.pf, 65535)
    elif l in PROXY:
        g.wait_ge(T.sem.parr, 8)
        sent += fold(g, core, T, topo, 8 * (c ^ 1) + FIN, [T.pland[j] for j in range(4)], T.part[2 + PROXY.index(l)], T.sem.pf, 255)
    elif l == FIN:
        g.wait_ge(T.sem.pf, 64)
        sent += fold(g, core, T, topo, 8 * c + 3, [T.part[j] for j in range(6)], T.fin[:], T.sem.af, 65535)
    g.wait_ge(T.sem.sent, sent)
    if l == 3:
        g.wait_ge(T.sem.st, 16)
